import numpy as np
import ml_dtypes


def mxq(x, axis, fmt="e4m3"):
    dtype, down = {"e4m3": (ml_dtypes.float8_e4m3fn, 7), "e5m2": (ml_dtypes.float8_e5m2, 14)}[fmt]
    v = np.moveaxis(np.asarray(x, np.float32).astype(ml_dtypes.bfloat16).astype(np.float64), axis, -1)
    blocks = v.reshape(v.shape[:-1] + (-1, 32))
    amax = np.abs(blocks).max(-1, keepdims=True)
    byte = np.maximum(np.where(amax > 0, np.frexp(amax)[1] - 1 + 127, 0) - down, 1)
    scale = np.exp2(byte - 127.0)
    codes = (blocks / scale).astype(np.float32).astype(dtype).astype(np.float64)
    return np.moveaxis((codes * scale).reshape(v.shape), -1, axis)


WIDE = False


def mx_kscale(k):
    if not WIDE:
        return np.ones(k)
    levels = np.array([10, -10, 5, -5, 0])
    if k % 512:
        return np.exp2(np.random.permutation(np.resize(levels, k // 32))).repeat(32)
    a = np.empty((k // 512, 16))
    for p in range(k // 512):
        a[p, :8] = np.random.permutation(np.resize(levels, 8))
        for g in range(8):
            far = levels[np.abs(levels - a[p, g]) >= 10]
            a[p, g + 8] = far[np.random.randint(len(far))]
    return np.exp2(a.ravel()).repeat(32)


def f64(x):
    return np.asarray(x).astype(np.float64)


def striped(idx):
    return np.tile(np.asarray(idx).reshape(-1, 16).T, (8, 1)).astype(np.uint16)


def unstriped(offs):
    return offs[:16].T.reshape(-1).astype(np.int64)


E2M1 = np.array([0.0, 0.5, 1.0, 1.5, 2.0, 3.0, 4.0, 6.0, -0.0, -0.5, -1.0, -1.5, -2.0, -3.0, -4.0, -6.0])


def pack_weight(w, fmt):
    k, n = w.shape
    w = f64(np.asarray(w, np.float32).astype(ml_dtypes.bfloat16)).reshape(k // 32, 32, n)
    amax = np.abs(w).max(1)
    if fmt == "e4m3":
        byte = np.frexp(amax)[1] - 1 + 127 - 7
    else:
        mant, ex = np.frexp(amax / 6.0)
        byte = np.where(mant > 0.5, ex, ex - 1) + 127
    byte = np.clip(np.where(amax > 0, byte, 1), 1, 254)
    scaled = (w * np.exp2(127.0 - byte)[:, None, :]).reshape(k, n).astype(np.float32)
    by_word = np.ascontiguousarray(scaled.reshape(k // 512, 128, 4, n).transpose(0, 1, 3, 2))
    if fmt == "e4m3":
        words = by_word.astype(ml_dtypes.float8_e4m3fn).view(np.uint8)
    else:
        c = by_word.astype(ml_dtypes.float4_e2m1fn).view(np.uint8) & 0xF
        words = (c[..., 0::2] | (c[..., 1::2] << 4)).reshape(k // 512, 128, 2 * n)
    return np.ascontiguousarray(words), np.ascontiguousarray(byte.astype(np.uint8).reshape(k // 512, 16, n))


def unpack_weight(words, scales, fmt):
    g, _, n = scales.shape
    words = np.ascontiguousarray(words).reshape(g, 128, n, -1)
    if fmt == "e4m3":
        vals = words.view(ml_dtypes.float8_e4m3fn).astype(np.float64)
    else:
        nib = np.empty((g, 128, n, 4), np.uint8)
        nib[..., 0::2] = words & 0xF
        nib[..., 1::2] = words >> 4
        vals = E2M1[nib]
    vals = vals * np.repeat(np.exp2(scales.astype(np.float64) - 127.0), 8, axis=1)[..., None]
    return vals.transpose(0, 1, 3, 2).reshape(g * 512, n)


D, T, I, J, U, E, N = 512, 2048, 512, 512, 1024, 512, 64


def setup_inputs():
    n = np.random.standard_normal
    idx = np.random.permutation(T)[:I]
    idx2 = np.random.permutation(U)[:J]
    idx3 = np.random.permutation(U)[:J]
    idx4 = np.random.permutation(U)[:J]
    fd = mx_kscale(D)
    fi = mx_kscale(I)
    ti = np.ones(T)
    ti[idx] = fi
    keysp = pack_weight(n((D, T)) / fd[:, None], "e4m3")
    return {
        "keys_words": keysp[0],
        "keys_scales": keysp[1],
        "notes": (n((D, U)) * 1.0 / np.sqrt(D) * fd[:, None]).astype(np.float32),
        "rowf": (np.random.uniform(0.02, 0.08, (I, 1)) * fi[:, None]).astype(np.float32),
        "vals": (n((E, T)) / ti).astype(np.float32),
        "offs": striped(idx),
        "offs2": striped(idx2),
        "offs3": striped(idx3),
        "offs4": striped(idx4),
    }


def reference(keys_words, keys_scales, notes, rowf, vals, offs, offs2, offs3, offs4):
    idx = unstriped(offs)
    idx2 = unstriped(offs2)
    idx3 = unstriped(offs3)
    idx4 = unstriped(offs4)
    keysu = unpack_weight(keys_words, keys_scales, "e4m3")
    keysidxg = keysu[:, idx]
    notesq = mxq(f64(notes), 0, "e4m3")
    g1 = keysidxg.T @ notesq
    lo2 = np.minimum(g1[:, idx2], g1[:, idx3])
    hi2 = np.maximum(g1[:, idx2], g1[:, idx3])
    g0 = np.maximum(lo2, np.minimum(hi2, g1[:, idx4]))
    gr1 = g0 * f64(rowf)
    vt1 = f64(vals)[:, idx].T
    vt1q = mxq(vt1, 0, "e4m3")
    gr1q = mxq(gr1, 0, "e4m3")
    o = vt1q.T @ gr1q
    y = o.reshape(E, N, J // N).max(axis=2)
    return y

@@ -1,0 +1,182 @@
+from contextlib import ExitStack
+
+import concourse.mybir as mybir
+from concourse.masks import make_identity
+
+F32 = mybir.dt.float32
+BF16 = mybir.dt.bfloat16
+I32 = mybir.dt.int32
+U32 = mybir.dt.uint32
+U16 = mybir.dt.uint16
+U8 = mybir.dt.uint8
+FP8X4 = mybir.dt.float8_e4m3fn_x4
+ALU = mybir.AluOpType
+COPY = mybir.ActivationFunctionType.Copy
+
+P = 128
+PACK = 4
+D, T, I, J, U, E, RUN = 512, 2048, 512, 512, 1024, 512, 8
+NOTE_CHUNK = 256
+
+FLOPS = 2 * D * I * U + 2 * I * E * J
+
+
+def tile_attend_tab_middleof3_bestruns_kernel(
+    tc, keys_words, keys_scales, notes, rowf, vals, offs, offs2, offs3, offs4, out
+):
+    nc = tc.nc
+    with ExitStack() as ctx:
+        held = ctx.enter_context(tc.tile_pool(name="held", bufs=1))
+        psum = ctx.enter_context(tc.psum_pool(name="psum", bufs=8))
+
+        def sb(shape, dtype, name):
+            return held.tile(shape, dtype, name=name, align_bytes=64)
+
+        def bank(name):
+            return psum.tile([P, 512], F32, name=name, tag="bank")
+
+        def gather(engine, dst, window, offsets):
+            if engine == "vector":
+                nc.vector.tensor_copy(dst, window.indirect(offsets))
+            else:
+                nc.scalar.activation(dst, window.indirect(offsets), COPY)
+
+        token_list = sb([P, I // 16], U16, "token_list")
+        nc.sync.dma_start(token_list[:], offs)
+
+        key_scales = sb([P, T], U8, "key_scales")
+        nc.vector.memset(key_scales[:].bitcast(I32), 0)
+        for q in range(4):
+            nc.scalar.dma_start(
+                key_scales[32 * q : 32 * q + 4, :].bitcast(I32),
+                keys_scales[0, 4 * q : 4 * q + 4, :].bitcast(I32),
+            )
+        key_words = sb([P, T], U32, "key_words")
+        nc.sync.dma_start(
+            key_words[:].bitcast(I32), keys_words[0].rearrange("p n t -> p (n t)").bitcast(I32)
+        )
+        notes_rows = notes.rearrange("(p t) u -> p t u", t=PACK)
+        note_raw = []
+        for c in range(U // NOTE_CHUNK):
+            raw = sb([P, PACK, NOTE_CHUNK], F32, f"note_raw{c}")
+            nc.sync.dma_start(raw[:], notes_rows[:, :, c * NOTE_CHUNK : (c + 1) * NOTE_CHUNK])
+            note_raw.append(raw)
+        note_lists = []
+        for k, src in enumerate((offs2, offs3, offs4)):
+            lst = sb([P, J // 16], U16, f"note_list{k}")
+            nc.sync.dma_start(lst[:], src)
+            note_lists.append(lst)
+        row_factor = sb([P, PACK], F32, "row_factor")
+        nc.sync.dma_start(row_factor[:], rowf.rearrange("(p t) one -> p (t one)", t=PACK))
+        vals_rows = vals.rearrange("(p b) t -> p b t", b=PACK)
+        val_pool = []
+        for b in range(PACK):
+            plane = sb([P, T], F32, f"val_pool{b}")
+            nc.sync.dma_start(plane[:], vals_rows[:, b, :])
+            val_pool.append(plane)
+
+        ident = sb([P, P], F32, "ident")
+        make_identity(nc, ident[:])
+
+        picked_scales = sb([P, I], U8, "picked_scales")
+        picked_words = sb([P, I], U32, "picked_words")
+        nc.vector.tensor_copy(
+            picked_scales[:].rearrange("p (r s) -> p s r", r=PACK), key_scales[:].indirect(token_list[:])
+        )
+        nc.vector.tensor_copy(
+            picked_words[:].rearrange("p (r s) -> p s r", r=PACK), key_words[:].indirect(token_list[:])
+        )
+
+        wide = [sb([P, U], F32, f"wide{r}") for r in range(PACK)]
+        chunks = U // NOTE_CHUNK
+        for c in range(chunks):
+            grouped = sb([P, NOTE_CHUNK, PACK], BF16, f"note_grouped{c}")
+            dst = grouped[:].rearrange("p (c i) t -> p c t i", i=4)
+            src = note_raw[c][:].rearrange("p t (c i) -> p c t i", i=4)
+            if c == 0:
+                nc.scalar.copy(dst, src)
+            else:
+                nc.vector.tensor_copy(dst, src)
+            codes = sb([P, NOTE_CHUNK], U32, f"note_codes{c}")
+            scales = sb([P, NOTE_CHUNK], U8, f"note_scales{c}")
+            nc.vector.quantize_mx(
+                out=codes[:].bitcast(FP8X4), scales=scales[:], in_=grouped[:].rearrange("p w t -> p (w t)")
+            )
+            for pair in range(2):
+                acc = bank(f"wide_acc{c}_{pair}")
+                for h in range(2):
+                    r = 2 * pair + h
+                    nc.tensor.matmul_mx(
+                        out=acc[:, h * NOTE_CHUNK : (h + 1) * NOTE_CHUNK],
+                        lhsT=picked_words[:, r * P : (r + 1) * P].bitcast(FP8X4),
+                        lhsT_scale=picked_scales[:, r * P : (r + 1) * P],
+                        rhs=codes[:].bitcast(FP8X4),
+                        rhs_scale=scales[:],
+                        start=True,
+                        stop=True,
+                    )
+                for h in range(2):
+                    r = 2 * pair + h
+                    dst = wide[r][:, c * NOTE_CHUNK : (c + 1) * NOTE_CHUNK]
+                    src = acc[:, h * NOTE_CHUNK : (h + 1) * NOTE_CHUNK]
+                    if c == chunks - 1 and pair == 0:
+                        nc.vector.tensor_copy(dst, src)
+                    else:
+                        nc.scalar.copy(dst, src)
+
+        middle = sb([P, PACK, J], F32, "middle")
+        on_vector = {(0, 0), (0, 1), (3, 0)}
+        for r in range(PACK):
+            picked = [sb([P, J], F32, f"picked{r}_{k}") for k in range(3)]
+            for k in range(3):
+                gather("vector" if (r, k) in on_vector else "scalar", picked[k][:], wide[r][:], note_lists[k][:])
+            hi = sb([P, J], F32, f"hi{r}")
+            lo = sb([P, J], F32, f"lo{r}")
+            nc.vector.tensor_tensor(hi[:], picked[0][:], picked[1][:], ALU.max)
+            nc.vector.tensor_tensor(lo[:], picked[0][:], picked[1][:], ALU.min)
+            nc.vector.tensor_tensor(hi[:], hi[:], picked[2][:], ALU.min)
+            nc.vector.tensor_tensor(middle[:, r, :], lo[:], hi[:], ALU.max)
+
+        table = sb([P, J, PACK], BF16, "table")
+        nc.vector.tensor_tensor(
+            table[:].rearrange("p (c i) t -> p c t i", i=4),
+            middle[:].rearrange("p t (c i) -> p c t i", i=4),
+            row_factor[:].rearrange("p (c t i) -> p c t i", c=1, i=1).to_broadcast([P, J // 4, PACK, 4]),
+            ALU.mult,
+        )
+        table_codes = sb([P, J], U32, "table_codes")
+        table_scales = sb([P, J], U8, "table_scales")
+        nc.vector.quantize_mx(
+            out=table_codes[:].bitcast(FP8X4), scales=table_scales[:], in_=table[:].rearrange("p w t -> p (w t)")
+        )
+
+        result = sb([P, PACK, J // RUN], F32, "result")
+        for b in range(PACK):
+            picked_vals = sb([P, I], BF16, f"picked_vals{b}")
+            gather("scalar", picked_vals[:], val_pool[b][:], token_list[:])
+            pairs = picked_vals[:].bitcast(F32)
+            turned = bank(f"turned{b}")
+            for u in range(2):
+                nc.tensor.transpose(turned[:, u * P : (u + 1) * P], pairs[:, u : I // 2 : 2], ident[:])
+            val_grouped = sb([P, P * PACK], BF16, f"val_grouped{b}")
+            nc.scalar.copy(
+                val_grouped[:].bitcast(F32).rearrange("p (e u) -> p e u", u=2),
+                turned[:, 0 : 2 * P].rearrange("p (u e) -> p e u", u=2),
+            )
+            val_codes = sb([P, P], U32, f"val_codes{b}")
+            val_scales = sb([P, P], U8, f"val_scales{b}")
+            nc.vector.quantize_mx(out=val_codes[:].bitcast(FP8X4), scales=val_scales[:], in_=val_grouped[:])
+            acc = bank(f"out_acc{b}")
+            nc.tensor.matmul_mx(
+                out=acc[:],
+                lhsT=val_codes[:].bitcast(FP8X4),
+                lhsT_scale=val_scales[:],
+                rhs=table_codes[:].bitcast(FP8X4),
+                rhs_scale=table_scales[:],
+                start=True,
+                stop=True,
+            )
+            nc.vector.tensor_reduce(
+                result[:, b, :], acc[:].rearrange("p (n k) -> p n k", k=RUN), mybir.AxisListType.X, ALU.max
+            )
+        nc.sync.dma_start(out.rearrange("(p b) n -> p b n", b=PACK), result[:])

@@ -29,8 +29,8 @@ def tile_attend_tab_middleof3_bestruns_kernel(
         held = ctx.enter_context(tc.tile_pool(name="held", bufs=1))
         psum = ctx.enter_context(tc.psum_pool(name="psum", bufs=8))
 
-        def sb(shape, dtype, name):
-            return held.tile(shape, dtype, name=name, align_bytes=64)
+        def sb(shape, dtype, name, tag=""):
+            return held.tile(shape, dtype, name=name, tag=tag or name, align_bytes=64)
 
         def bank(name):
             return psum.tile([P, 512], F32, name=name, tag="bank")
@@ -46,8 +46,17 @@ def tile_attend_tab_middleof3_bestruns_kernel(
 
         key_scales = sb([P, T], U8, "key_scales")
         nc.vector.memset(key_scales[:].bitcast(I32), 0)
+        notes_rows = notes.rearrange("(p t) u -> p t u", t=PACK)
+        note_raw = []
+
+        def load_notes(c):
+            raw = sb([P, PACK, NOTE_CHUNK], F32, f"note_raw{c}")
+            nc.sync.dma_start(raw[:], notes_rows[:, :, c * NOTE_CHUNK : (c + 1) * NOTE_CHUNK])
+            note_raw.append(raw)
+
+        load_notes(0)
         for q in range(4):
-            nc.scalar.dma_start(
+            nc.sync.dma_start(
                 key_scales[32 * q : 32 * q + 4, :].bitcast(I32),
                 keys_scales[0, 4 * q : 4 * q + 4, :].bitcast(I32),
             )
@@ -55,12 +64,8 @@ def tile_attend_tab_middleof3_bestruns_kernel(
         nc.sync.dma_start(
             key_words[:].bitcast(I32), keys_words[0].rearrange("p n t -> p (n t)").bitcast(I32)
         )
-        notes_rows = notes.rearrange("(p t) u -> p t u", t=PACK)
-        note_raw = []
-        for c in range(U // NOTE_CHUNK):
-            raw = sb([P, PACK, NOTE_CHUNK], F32, f"note_raw{c}")
-            nc.sync.dma_start(raw[:], notes_rows[:, :, c * NOTE_CHUNK : (c + 1) * NOTE_CHUNK])
-            note_raw.append(raw)
+        for c in range(1, U // NOTE_CHUNK):
+            load_notes(c)
         note_lists = []
         for k, src in enumerate((offs2, offs3, offs4)):
             lst = sb([P, J // 16], U16, f"note_list{k}")
@@ -78,30 +83,27 @@ def tile_attend_tab_middleof3_bestruns_kernel(
         ident = sb([P, P], F32, "ident")
         make_identity(nc, ident[:])
 
-        picked_scales = sb([P, I], U8, "picked_scales")
-        picked_words = sb([P, I], U32, "picked_words")
-        nc.vector.tensor_copy(
-            picked_scales[:].rearrange("p (r s) -> p s r", r=PACK), key_scales[:].indirect(token_list[:])
-        )
-        nc.vector.tensor_copy(
-            picked_words[:].rearrange("p (r s) -> p s r", r=PACK), key_words[:].indirect(token_list[:])
-        )
-
         wide = [sb([P, U], F32, f"wide{r}") for r in range(PACK)]
         chunks = U // NOTE_CHUNK
+        picked_scales = sb([P, I], U8, "picked_scales")
+        picked_words = sb([P, I], U32, "picked_words")
         for c in range(chunks):
-            grouped = sb([P, NOTE_CHUNK, PACK], BF16, f"note_grouped{c}")
+            grouped = sb([P, NOTE_CHUNK, PACK], BF16, f"note_grouped{c}", tag="note_raw1" if c == 2 else "note_grouped")
             dst = grouped[:].rearrange("p (c i) t -> p c t i", i=4)
             src = note_raw[c][:].rearrange("p t (c i) -> p c t i", i=4)
-            if c == 0:
-                nc.scalar.copy(dst, src)
-            else:
-                nc.vector.tensor_copy(dst, src)
+            nc.vector.tensor_copy(dst, src)
             codes = sb([P, NOTE_CHUNK], U32, f"note_codes{c}")
             scales = sb([P, NOTE_CHUNK], U8, f"note_scales{c}")
             nc.vector.quantize_mx(
                 out=codes[:].bitcast(FP8X4), scales=scales[:], in_=grouped[:].rearrange("p w t -> p (w t)")
             )
+            if c == 0:
+                nc.vector.tensor_copy(
+                    picked_scales[:].rearrange("p (r s) -> p s r", r=PACK), key_scales[:].indirect(token_list[:])
+                )
+                nc.vector.tensor_copy(
+                    picked_words[:].rearrange("p (r s) -> p s r", r=PACK), key_words[:].indirect(token_list[:])
+                )
             for pair in range(2):
                 acc = bank(f"wide_acc{c}_{pair}")
                 for h in range(2):
@@ -119,13 +121,13 @@ def tile_attend_tab_middleof3_bestruns_kernel(
                     r = 2 * pair + h
                     dst = wide[r][:, c * NOTE_CHUNK : (c + 1) * NOTE_CHUNK]
                     src = acc[:, h * NOTE_CHUNK : (h + 1) * NOTE_CHUNK]
-                    if c == chunks - 1 and pair == 0:
+                    if (c, pair) in ((chunks - 2, 0), (chunks - 1, 0)):
                         nc.vector.tensor_copy(dst, src)
                     else:
                         nc.scalar.copy(dst, src)
 
         middle = sb([P, PACK, J], F32, "middle")
-        on_vector = {(0, 0), (0, 1), (3, 0)}
+        on_vector = {(0, 0), (0, 1), (1, 0)}
         for r in range(PACK):
             picked = [sb([P, J], F32, f"picked{r}_{k}") for k in range(3)]
             for k in range(3):
@@ -151,26 +153,37 @@ def tile_attend_tab_middleof3_bestruns_kernel(
         )
 
         result = sb([P, PACK, J // RUN], F32, "result")
+        val_codes = sb([P, 2 * P], U32, "val_codes", tag="middle")
+        val_scales = sb([P, 2 * P], U8, "val_scales")
+        val_grouped = []
         for b in range(PACK):
-            picked_vals = sb([P, I], BF16, f"picked_vals{b}")
+            picked_vals = sb([P, I], BF16, f"picked_vals{b}", tag=("picked2_0", "picked2_1", "picked2_2", "picked3_0")[b])
             gather("scalar", picked_vals[:], val_pool[b][:], token_list[:])
             pairs = picked_vals[:].bitcast(F32)
             turned = bank(f"turned{b}")
             for u in range(2):
                 nc.tensor.transpose(turned[:, u * P : (u + 1) * P], pairs[:, u : I // 2 : 2], ident[:])
-            val_grouped = sb([P, P * PACK], BF16, f"val_grouped{b}")
+            grouped = sb([P, P * PACK], BF16, f"val_grouped{b}")
             nc.scalar.copy(
-                val_grouped[:].bitcast(F32).rearrange("p (e u) -> p e u", u=2),
+                grouped[:].bitcast(F32).rearrange("p (e u) -> p e u", u=2),
                 turned[:, 0 : 2 * P].rearrange("p (u e) -> p e u", u=2),
             )
-            val_codes = sb([P, P], U32, f"val_codes{b}")
-            val_scales = sb([P, P], U8, f"val_scales{b}")
-            nc.vector.quantize_mx(out=val_codes[:].bitcast(FP8X4), scales=val_scales[:], in_=val_grouped[:])
+            val_grouped.append(grouped)
+
+        def slot(b):
+            return slice(b % 2 * P, (b % 2 + 1) * P)
+
+        def quantize_vals(b):
+            nc.vector.quantize_mx(
+                out=val_codes[:, slot(b)].bitcast(FP8X4), scales=val_scales[:, slot(b)], in_=val_grouped[b][:]
+            )
+
+        def product_and_maxima(b):
             acc = bank(f"out_acc{b}")
             nc.tensor.matmul_mx(
                 out=acc[:],
-                lhsT=val_codes[:].bitcast(FP8X4),
-                lhsT_scale=val_scales[:],
+                lhsT=val_codes[:, slot(b)].bitcast(FP8X4),
+                lhsT_scale=val_scales[:, slot(b)],
                 rhs=table_codes[:].bitcast(FP8X4),
                 rhs_scale=table_scales[:],
                 start=True,
@@ -179,4 +192,11 @@ def tile_attend_tab_middleof3_bestruns_kernel(
             nc.vector.tensor_reduce(
                 result[:, b, :], acc[:].rearrange("p (n k) -> p n k", k=RUN), mybir.AxisListType.X, ALU.max
             )
+
+        quantize_vals(0)
+        quantize_vals(1)
+        for b in range(PACK):
+            product_and_maxima(b)
+            if b + 2 < PACK:
+                quantize_vals(b + 2)
         nc.sync.dma_start(out.rearrange("(p b) n -> p b n", b=PACK), result[:])

@@ -27,13 +27,13 @@ def tile_attend_tab_middleof3_bestruns_kernel(
     nc = tc.nc
     with ExitStack() as ctx:
         held = ctx.enter_context(tc.tile_pool(name="held", bufs=1))
-        psum = ctx.enter_context(tc.psum_pool(name="psum", bufs=8))
+        psum = ctx.enter_context(tc.psum_pool(name="psum", bufs=1))
 
         def sb(shape, dtype, name, tag=""):
             return held.tile(shape, dtype, name=name, tag=tag or name, align_bytes=64)
 
-        def bank(name):
-            return psum.tile([P, 512], F32, name=name, tag="bank")
+        def bank(name, number):
+            return psum.tile([P, 512], F32, name=name, tag=f"bank{number}")
 
         def gather(engine, dst, window, offsets):
             if engine == "vector":
@@ -104,10 +104,14 @@ def tile_attend_tab_middleof3_bestruns_kernel(
                 nc.vector.tensor_copy(
                     picked_words[:].rearrange("p (r s) -> p s r", r=PACK), key_words[:].indirect(token_list[:])
                 )
-            for pair in range(2):
-                acc = bank(f"wide_acc{c}_{pair}")
-                for h in range(2):
-                    r = 2 * pair + h
+            groups = [((0, 1), 2 * c), ((2, 3), 2 * c + 1)]
+            if c == chunks - 2:
+                groups = [((0, 1), 4), ((2, 3), 4)]
+            if c == chunks - 1:
+                groups = [((0,), 5), ((1,), 6), ((2, 3), 7)]
+            for rows, number in groups:
+                acc = bank(f"wide_acc{c}_{rows[0]}", number)
+                for h, r in enumerate(rows):
                     nc.tensor.matmul_mx(
                         out=acc[:, h * NOTE_CHUNK : (h + 1) * NOTE_CHUNK],
                         lhsT=picked_words[:, r * P : (r + 1) * P].bitcast(FP8X4),
@@ -117,61 +121,104 @@ def tile_attend_tab_middleof3_bestruns_kernel(
                         start=True,
                         stop=True,
                     )
-                for h in range(2):
-                    r = 2 * pair + h
+                for h, r in enumerate(rows):
                     dst = wide[r][:, c * NOTE_CHUNK : (c + 1) * NOTE_CHUNK]
                     src = acc[:, h * NOTE_CHUNK : (h + 1) * NOTE_CHUNK]
-                    if (c, pair) in ((chunks - 2, 0), (chunks - 1, 0)):
+                    if c >= chunks - 2 and r < 2:
                         nc.vector.tensor_copy(dst, src)
                     else:
                         nc.scalar.copy(dst, src)
 
-        middle = sb([P, PACK, J], F32, "middle")
-        on_vector = {(0, 0), (0, 1), (1, 0)}
+        first = [sb([P, J], F32, f"first{r}") for r in range(PACK)]
+        second = [sb([P, J], F32, f"second{r}") for r in range(PACK)]
+        third = [sb([P, J], F32, f"third{r}") for r in range(PACK)]
+        scaled = [sb([P, J], F32, f"scaled{r}") for r in range(PACK)]
+        upper = [sb([P, J], F32, f"upper{r}") for r in range(PACK)]
+        lower = sb([P, PACK, J], F32, "lower")
+        capped = sb([P, PACK, J], F32, "capped")
+        halves = (slice(0, J // 2), slice(J // 2, J))
+
+        def look_up(engine, dst, r, k, cols=slice(0, J)):
+            gather(engine, dst[r][:, cols], wide[r][:], note_lists[k][:, cols.start // 16 : cols.stop // 16])
+
+        def scale_second(r):
+            nc.vector.tensor_scalar(scaled[r][:], second[r][:], row_factor[:, r : r + 1], None, ALU.mult)
+
+        def scaled_against(dst, src, r, other, op):
+            nc.vector.scalar_tensor_tensor(dst, src, row_factor[:, r : r + 1], other, ALU.mult, op)
+
+        look_up("vector", second, 0, 1)
+        look_up("vector", first, 0, 0)
+        scale_second(0)
+        look_up("vector", second, 1, 1)
+        look_up("vector", first, 1, 0)
+        look_up("vector", third, 1, 2, halves[0])
+        look_up("scalar", third, 0, 2)
+        look_up("scalar", third, 1, 2, halves[1])
+        for r in (2, 3):
+            look_up("scalar", second, r, 1)
+            look_up("scalar", first, r, 0)
+            look_up("scalar", third, r, 2)
         for r in range(PACK):
-            picked = [sb([P, J], F32, f"picked{r}_{k}") for k in range(3)]
-            for k in range(3):
-                gather("vector" if (r, k) in on_vector else "scalar", picked[k][:], wide[r][:], note_lists[k][:])
-            hi = sb([P, J], F32, f"hi{r}")
-            lo = sb([P, J], F32, f"lo{r}")
-            nc.vector.tensor_tensor(hi[:], picked[0][:], picked[1][:], ALU.max)
-            nc.vector.tensor_tensor(lo[:], picked[0][:], picked[1][:], ALU.min)
-            nc.vector.tensor_tensor(hi[:], hi[:], picked[2][:], ALU.min)
-            nc.vector.tensor_tensor(middle[:, r, :], lo[:], hi[:], ALU.max)
+            scaled_against(upper[r][:], first[r][:], r, scaled[r][:], ALU.max)
+            scaled_against(lower[:, r, :], first[r][:], r, scaled[r][:], ALU.min)
+            if r + 1 < PACK:
+                scale_second(r + 1)
+                scaled_against(capped[:, r, :], third[r][:], r, upper[r][:], ALU.min)
+            else:
+                for cols in halves:
+                    scaled_against(capped[:, r, cols], third[r][:, cols], r, upper[r][:, cols], ALU.min)
 
         table = sb([P, J, PACK], BF16, "table")
-        nc.vector.tensor_tensor(
-            table[:].rearrange("p (c i) t -> p c t i", i=4),
-            middle[:].rearrange("p t (c i) -> p c t i", i=4),
-            row_factor[:].rearrange("p (c t i) -> p c t i", c=1, i=1).to_broadcast([P, J // 4, PACK, 4]),
-            ALU.mult,
-        )
+        for cols in halves:
+            nc.vector.tensor_tensor(
+                table[:, cols, :].rearrange("p (c i) t -> p c t i", i=4),
+                lower[:, :, cols].rearrange("p t (c i) -> p c t i", i=4),
+                capped[:, :, cols].rearrange("p t (c i) -> p c t i", i=4),
+                ALU.max,
+            )
         table_codes = sb([P, J], U32, "table_codes")
         table_scales = sb([P, J], U8, "table_scales")
-        nc.vector.quantize_mx(
-            out=table_codes[:].bitcast(FP8X4), scales=table_scales[:], in_=table[:].rearrange("p w t -> p (w t)")
-        )
+
+        def quantize_table(cols):
+            nc.vector.quantize_mx(
+                out=table_codes[:, cols].bitcast(FP8X4),
+                scales=table_scales[:, cols],
+                in_=table[:, cols, :].rearrange("p w t -> p (w t)"),
+            )
 
         result = sb([P, PACK, J // RUN], F32, "result")
-        val_codes = sb([P, 2 * P], U32, "val_codes", tag="middle")
-        val_scales = sb([P, 2 * P], U8, "val_scales")
+        val_codes = sb([P, E], U32, "val_codes", tag="lower")
+        val_scales = sb([P, E], U8, "val_scales")
+        picked_vals = []
         val_grouped = []
-        for b in range(PACK):
-            picked_vals = sb([P, I], BF16, f"picked_vals{b}", tag=("picked2_0", "picked2_1", "picked2_2", "picked3_0")[b])
-            gather("scalar", picked_vals[:], val_pool[b][:], token_list[:])
-            pairs = picked_vals[:].bitcast(F32)
-            turned = bank(f"turned{b}")
+
+        def gather_vals(b):
+            picked = sb([P, I], BF16, f"picked_vals{b}", tag=("first0", "scaled0", "third0", "upper0")[b])
+            gather("scalar", picked[:], val_pool[b][:], token_list[:])
+            picked_vals.append(picked)
+
+        def turn_vals(b):
+            pairs = picked_vals[b][:].bitcast(F32)
+            turned = bank(f"turned{b}", b)
             for u in range(2):
                 nc.tensor.transpose(turned[:, u * P : (u + 1) * P], pairs[:, u : I // 2 : 2], ident[:])
-            grouped = sb([P, P * PACK], BF16, f"val_grouped{b}")
+            grouped = sb([P, P * PACK], BF16, f"val_grouped{b}", tag="val_pool3" if b == 2 else "")
             nc.scalar.copy(
                 grouped[:].bitcast(F32).rearrange("p (e u) -> p e u", u=2),
                 turned[:, 0 : 2 * P].rearrange("p (u e) -> p e u", u=2),
             )
             val_grouped.append(grouped)
 
+        gather_vals(0)
+        gather_vals(1)
+        for b in range(PACK):
+            if b + 2 < PACK:
+                gather_vals(b + 2)
+            turn_vals(b)
+
         def slot(b):
-            return slice(b % 2 * P, (b % 2 + 1) * P)
+            return slice(b * P, (b + 1) * P)
 
         def quantize_vals(b):
             nc.vector.quantize_mx(
@@ -179,24 +226,27 @@ def tile_attend_tab_middleof3_bestruns_kernel(
             )
 
         def product_and_maxima(b):
-            acc = bank(f"out_acc{b}")
-            nc.tensor.matmul_mx(
-                out=acc[:],
-                lhsT=val_codes[:, slot(b)].bitcast(FP8X4),
-                lhsT_scale=val_scales[:, slot(b)],
-                rhs=table_codes[:].bitcast(FP8X4),
-                rhs_scale=table_scales[:],
-                start=True,
-                stop=True,
-            )
+            acc = bank(f"out_acc{b}", PACK + b)
+            for cols in halves if b == 0 else (slice(0, J),):
+                nc.tensor.matmul_mx(
+                    out=acc[:, cols],
+                    lhsT=val_codes[:, slot(b)].bitcast(FP8X4),
+                    lhsT_scale=val_scales[:, slot(b)],
+                    rhs=table_codes[:, cols].bitcast(FP8X4),
+                    rhs_scale=table_scales[:, cols],
+                    start=True,
+                    stop=True,
+                )
             nc.vector.tensor_reduce(
                 result[:, b, :], acc[:].rearrange("p (n k) -> p n k", k=RUN), mybir.AxisListType.X, ALU.max
             )
 
+        quantize_table(halves[0])
         quantize_vals(0)
+        quantize_table(halves[1])
         quantize_vals(1)
+        quantize_vals(2)
+        quantize_vals(3)
         for b in range(PACK):
             product_and_maxima(b)
-            if b + 2 < PACK:
-                quantize_vals(b + 2)
         nc.sync.dma_start(out.rearrange("(p b) n -> p b n", b=PACK), result[:])

@@ -15,8 +15,14 @@ COPY = mybir.ActivationFunctionType.Copy
 
 P = 128
 PACK = 4
+QUADRANTS = 4
+LIST_ROWS = 16
 D, T, I, J, U, E, RUN = 512, 2048, 512, 512, 1024, 512, 8
+BANK = 512
 NOTE_CHUNK = 256
+CHUNKS = U // NOTE_CHUNK
+LINE = 4
+VECTOR_TILES = 2
 
 FLOPS = 2 * D * I * U + 2 * I * E * J
 
@@ -29,209 +35,209 @@ def tile_attend_tab_middleof3_bestruns_kernel(
         held = ctx.enter_context(tc.tile_pool(name="held", bufs=1))
         psum = ctx.enter_context(tc.psum_pool(name="psum", bufs=1))
 
-        def sb(shape, dtype, name, tag=""):
-            return held.tile(shape, dtype, name=name, tag=tag or name, align_bytes=64)
+        def sbuf(shape, dtype, name, reuse=""):
+            return held.tile(shape, dtype, name=name, tag=reuse or name, align_bytes=64)
 
         def bank(name, number):
-            return psum.tile([P, 512], F32, name=name, tag=f"bank{number}")
+            return psum.tile([P, BANK], F32, name=name, tag=f"bank{number}")
 
-        def gather(engine, dst, window, offsets):
-            if engine == "vector":
-                nc.vector.tensor_copy(dst, window.indirect(offsets))
-            else:
-                nc.scalar.activation(dst, window.indirect(offsets), COPY)
+        def vector_gather(dst, window, offsets):
+            nc.vector.tensor_copy(dst, window.indirect(offsets))
 
-        token_list = sb([P, I // 16], U16, "token_list")
-        nc.sync.dma_start(token_list[:], offs)
+        def scalar_gather(dst, window, offsets):
+            nc.scalar.activation(dst, window.indirect(offsets), COPY)
 
-        key_scales = sb([P, T], U8, "key_scales")
-        nc.vector.memset(key_scales[:].bitcast(I32), 0)
+        def by_place(planes):
+            return planes.rearrange("p t (c i) -> p c t i", i=LINE)
+
+        def into_words(grouped):
+            return grouped.rearrange("p (c i) t -> p c t i", i=LINE)
+
         notes_rows = notes.rearrange("(p t) u -> p t u", t=PACK)
         note_raw = []
 
         def load_notes(c):
-            raw = sb([P, PACK, NOTE_CHUNK], F32, f"note_raw{c}")
+            raw = sbuf([P, PACK, NOTE_CHUNK], F32, f"note_raw{c}")
             nc.sync.dma_start(raw[:], notes_rows[:, :, c * NOTE_CHUNK : (c + 1) * NOTE_CHUNK])
             note_raw.append(raw)
 
         load_notes(0)
-        for q in range(4):
+        token_list = sbuf([P, I // LIST_ROWS], U16, "token_list")
+        nc.sync.dma_start(token_list[:], offs)
+
+        key_scales = sbuf([P, T], U8, "key_scales")
+        nc.vector.memset(key_scales[:].bitcast(I32), 0)
+        for q in range(QUADRANTS):
             nc.sync.dma_start(
                 key_scales[32 * q : 32 * q + 4, :].bitcast(I32),
                 keys_scales[0, 4 * q : 4 * q + 4, :].bitcast(I32),
             )
-        key_words = sb([P, T], U32, "key_words")
+        key_words = sbuf([P, T], U32, "key_words")
         nc.sync.dma_start(
             key_words[:].bitcast(I32), keys_words[0].rearrange("p n t -> p (n t)").bitcast(I32)
         )
-        for c in range(1, U // NOTE_CHUNK):
+        for c in range(1, CHUNKS):
             load_notes(c)
         note_lists = []
-        for k, src in enumerate((offs2, offs3, offs4)):
-            lst = sb([P, J // 16], U16, f"note_list{k}")
-            nc.sync.dma_start(lst[:], src)
-            note_lists.append(lst)
-        row_factor = sb([P, PACK], F32, "row_factor")
+        for k, source in enumerate((offs2, offs3, offs4)):
+            note_list = sbuf([P, J // LIST_ROWS], U16, f"note_list{k}")
+            nc.sync.dma_start(note_list[:], source)
+            note_lists.append(note_list)
+        row_factor = sbuf([P, PACK], F32, "row_factor")
         nc.sync.dma_start(row_factor[:], rowf.rearrange("(p t) one -> p (t one)", t=PACK))
         vals_rows = vals.rearrange("(p b) t -> p b t", b=PACK)
         val_pool = []
         for b in range(PACK):
-            plane = sb([P, T], F32, f"val_pool{b}")
-            nc.sync.dma_start(plane[:], vals_rows[:, b, :])
-            val_pool.append(plane)
+            pool_block = sbuf([P, T], F32, f"val_pool{b}")
+            nc.sync.dma_start(pool_block[:], vals_rows[:, b, :])
+            val_pool.append(pool_block)
 
-        ident = sb([P, P], F32, "ident")
-        make_identity(nc, ident[:])
+        identity = sbuf([P, P], F32, "identity")
+        make_identity(nc, identity[:])
 
-        wide = [sb([P, U], F32, f"wide{r}") for r in range(PACK)]
-        chunks = U // NOTE_CHUNK
-        picked_scales = sb([P, I], U8, "picked_scales")
-        picked_words = sb([P, I], U32, "picked_words")
-        for c in range(chunks):
-            grouped = sb([P, NOTE_CHUNK, PACK], BF16, f"note_grouped{c}", tag="note_raw1" if c == 2 else "note_grouped")
-            dst = grouped[:].rearrange("p (c i) t -> p c t i", i=4)
-            src = note_raw[c][:].rearrange("p t (c i) -> p c t i", i=4)
-            nc.vector.tensor_copy(dst, src)
-            codes = sb([P, NOTE_CHUNK], U32, f"note_codes{c}")
-            scales = sb([P, NOTE_CHUNK], U8, f"note_scales{c}")
-            nc.vector.quantize_mx(
-                out=codes[:].bitcast(FP8X4), scales=scales[:], in_=grouped[:].rearrange("p w t -> p (w t)")
+        wide = [sbuf([P, U], F32, f"wide{t}") for t in range(PACK)]
+        picked_scales = sbuf([P, I], U8, "picked_scales")
+        picked_words = sbuf([P, I], U32, "picked_words")
+
+        def quantize_notes(c):
+            grouped = sbuf(
+                [P, NOTE_CHUNK, PACK], BF16, f"note_grouped{c}", reuse="note_raw1" if c == 2 else "note_grouped"
             )
-            if c == 0:
-                nc.vector.tensor_copy(
-                    picked_scales[:].rearrange("p (r s) -> p s r", r=PACK), key_scales[:].indirect(token_list[:])
-                )
-                nc.vector.tensor_copy(
-                    picked_words[:].rearrange("p (r s) -> p s r", r=PACK), key_words[:].indirect(token_list[:])
-                )
-            groups = [((0, 1), 2 * c), ((2, 3), 2 * c + 1)]
-            if c == chunks - 2:
-                groups = [((0, 1), 4), ((2, 3), 4)]
-            if c == chunks - 1:
-                groups = [((0,), 5), ((1,), 6), ((2, 3), 7)]
-            for rows, number in groups:
-                acc = bank(f"wide_acc{c}_{rows[0]}", number)
-                for h, r in enumerate(rows):
-                    nc.tensor.matmul_mx(
-                        out=acc[:, h * NOTE_CHUNK : (h + 1) * NOTE_CHUNK],
-                        lhsT=picked_words[:, r * P : (r + 1) * P].bitcast(FP8X4),
-                        lhsT_scale=picked_scales[:, r * P : (r + 1) * P],
-                        rhs=codes[:].bitcast(FP8X4),
-                        rhs_scale=scales[:],
-                        start=True,
-                        stop=True,
-                    )
-                for h, r in enumerate(rows):
-                    dst = wide[r][:, c * NOTE_CHUNK : (c + 1) * NOTE_CHUNK]
-                    src = acc[:, h * NOTE_CHUNK : (h + 1) * NOTE_CHUNK]
-                    if c >= chunks - 2 and r < 2:
-                        nc.vector.tensor_copy(dst, src)
-                    else:
-                        nc.scalar.copy(dst, src)
+            nc.vector.tensor_copy(into_words(grouped[:]), by_place(note_raw[c][:]))
+            codes = sbuf([P, NOTE_CHUNK], U32, f"note_codes{c}")
+            scales = sbuf([P, NOTE_CHUNK], U8, f"note_scales{c}")
+            nc.vector.quantize_mx(
+                out=codes[:].bitcast(FP8X4), scales=scales[:], in_=grouped[:].rearrange("p u t -> p (u t)")
+            )
+            return codes, scales
 
-        first = [sb([P, J], F32, f"first{r}") for r in range(PACK)]
-        second = [sb([P, J], F32, f"second{r}") for r in range(PACK)]
-        third = [sb([P, J], F32, f"third{r}") for r in range(PACK)]
-        scaled = [sb([P, J], F32, f"scaled{r}") for r in range(PACK)]
-        upper = [sb([P, J], F32, f"upper{r}") for r in range(PACK)]
-        lower = sb([P, PACK, J], F32, "lower")
-        capped = sb([P, PACK, J], F32, "capped")
+        def gather_keys():
+            vector_gather(picked_scales[:].rearrange("p (t s) -> p s t", t=PACK), key_scales[:], token_list[:])
+            vector_gather(picked_words[:].rearrange("p (t s) -> p s t", t=PACK), key_words[:], token_list[:])
+
+        def wide_columns(c, codes, scales, row_tiles, number, copy):
+            acc = bank(f"wide_acc{c}_{row_tiles[0]}", number)
+            for h, t in enumerate(row_tiles):
+                nc.tensor.matmul_mx(
+                    out=acc[:, h * NOTE_CHUNK : (h + 1) * NOTE_CHUNK],
+                    lhsT=picked_words[:, t * P : (t + 1) * P].bitcast(FP8X4),
+                    lhsT_scale=picked_scales[:, t * P : (t + 1) * P],
+                    rhs=codes[:].bitcast(FP8X4),
+                    rhs_scale=scales[:],
+                    start=True,
+                    stop=True,
+                )
+            for h, t in enumerate(row_tiles):
+                copy(wide[t][:, c * NOTE_CHUNK : (c + 1) * NOTE_CHUNK], acc[:, h * NOTE_CHUNK : (h + 1) * NOTE_CHUNK])
+
+        for c in range(2):
+            codes, scales = quantize_notes(c)
+            if c == 0:
+                gather_keys()
+            wide_columns(c, codes, scales, (0, 1), 2 * c, nc.scalar.copy)
+            wide_columns(c, codes, scales, (2, 3), 2 * c + 1, nc.scalar.copy)
+        codes, scales = quantize_notes(2)
+        wide_columns(2, codes, scales, (0, 1), 4, nc.vector.tensor_copy)
+        wide_columns(2, codes, scales, (2, 3), 4, nc.scalar.copy)
+        codes, scales = quantize_notes(3)
+        wide_columns(3, codes, scales, (0,), 5, nc.vector.tensor_copy)
+        wide_columns(3, codes, scales, (1,), 6, nc.vector.tensor_copy)
+        wide_columns(3, codes, scales, (2, 3), 7, nc.scalar.copy)
+
+        first = [sbuf([P, J], F32, f"first{t}") for t in range(PACK)]
+        second = [sbuf([P, J], F32, f"second{t}") for t in range(PACK)]
+        third = [sbuf([P, J], F32, f"third{t}") for t in range(PACK)]
+        scaled = [sbuf([P, J], F32, f"scaled{t}") for t in range(PACK)]
+        upper = [sbuf([P, J], F32, f"upper{t}") for t in range(PACK)]
+        lower = sbuf([P, PACK, J], F32, "lower")
+        capped = sbuf([P, PACK, J], F32, "capped")
         halves = (slice(0, J // 2), slice(J // 2, J))
 
-        def look_up(engine, dst, r, k, cols=slice(0, J)):
-            gather(engine, dst[r][:, cols], wide[r][:], note_lists[k][:, cols.start // 16 : cols.stop // 16])
+        def scale_second(t):
+            nc.vector.tensor_scalar(scaled[t][:], second[t][:], row_factor[:, t : t + 1], None, ALU.mult)
 
-        def scale_second(r):
-            nc.vector.tensor_scalar(scaled[r][:], second[r][:], row_factor[:, r : r + 1], None, ALU.mult)
+        def scale_and_compare(dst, looked_up, t, other, op):
+            nc.vector.scalar_tensor_tensor(dst, looked_up, row_factor[:, t : t + 1], other, ALU.mult, op)
 
-        def scaled_against(dst, src, r, other, op):
-            nc.vector.scalar_tensor_tensor(dst, src, row_factor[:, r : r + 1], other, ALU.mult, op)
-
-        look_up("vector", second, 0, 1)
-        look_up("vector", first, 0, 0)
-        scale_second(0)
-        look_up("vector", second, 1, 1)
-        look_up("vector", first, 1, 0)
-        look_up("vector", third, 1, 2, halves[0])
-        look_up("scalar", third, 0, 2)
-        look_up("scalar", third, 1, 2, halves[1])
-        for r in (2, 3):
-            look_up("scalar", second, r, 1)
-            look_up("scalar", first, r, 0)
-            look_up("scalar", third, r, 2)
-        for r in range(PACK):
-            scaled_against(upper[r][:], first[r][:], r, scaled[r][:], ALU.max)
-            scaled_against(lower[:, r, :], first[r][:], r, scaled[r][:], ALU.min)
-            if r + 1 < PACK:
-                scale_second(r + 1)
-                scaled_against(capped[:, r, :], third[r][:], r, upper[r][:], ALU.min)
+        for t in range(PACK):
+            gather = vector_gather if t < VECTOR_TILES else scalar_gather
+            gather(second[t][:], wide[t][:], note_lists[1][:])
+            gather(first[t][:], wide[t][:], note_lists[0][:])
+            if t == 0:
+                scale_second(t)
+            scalar_gather(third[t][:], wide[t][:], note_lists[2][:])
+        for t in range(PACK):
+            scale_and_compare(upper[t][:], first[t][:], t, scaled[t][:], ALU.max)
+            scale_and_compare(lower[:, t, :], first[t][:], t, scaled[t][:], ALU.min)
+            if t + 1 < PACK:
+                scale_second(t + 1)
+                scale_and_compare(capped[:, t, :], third[t][:], t, upper[t][:], ALU.min)
             else:
                 for cols in halves:
-                    scaled_against(capped[:, r, cols], third[r][:, cols], r, upper[r][:, cols], ALU.min)
-
-        table = sb([P, J, PACK], BF16, "table")
+                    scale_and_compare(capped[:, t, cols], third[t][:, cols], t, upper[t][:, cols], ALU.min)
+        table = sbuf([P, J, PACK], BF16, "table")
         for cols in halves:
             nc.vector.tensor_tensor(
-                table[:, cols, :].rearrange("p (c i) t -> p c t i", i=4),
-                lower[:, :, cols].rearrange("p t (c i) -> p c t i", i=4),
-                capped[:, :, cols].rearrange("p t (c i) -> p c t i", i=4),
-                ALU.max,
+                into_words(table[:, cols, :]), by_place(lower[:, :, cols]), by_place(capped[:, :, cols]), ALU.max
             )
-        table_codes = sb([P, J], U32, "table_codes")
-        table_scales = sb([P, J], U8, "table_scales")
+        table_codes = sbuf([P, J], U32, "table_codes")
+        table_scales = sbuf([P, J], U8, "table_scales")
 
         def quantize_table(cols):
             nc.vector.quantize_mx(
                 out=table_codes[:, cols].bitcast(FP8X4),
                 scales=table_scales[:, cols],
-                in_=table[:, cols, :].rearrange("p w t -> p (w t)"),
+                in_=table[:, cols, :].rearrange("p j t -> p (j t)"),
             )
 
-        result = sb([P, PACK, J // RUN], F32, "result")
-        val_codes = sb([P, E], U32, "val_codes", tag="lower")
-        val_scales = sb([P, E], U8, "val_scales")
         picked_vals = []
-        val_grouped = []
 
         def gather_vals(b):
-            picked = sb([P, I], BF16, f"picked_vals{b}", tag=("first0", "scaled0", "third0", "upper0")[b])
-            gather("scalar", picked[:], val_pool[b][:], token_list[:])
+            picked = sbuf([P, I], BF16, f"picked_vals{b}", reuse=("first0", "scaled0", "third0", "upper0")[b])
+            scalar_gather(picked[:], val_pool[b][:], token_list[:])
             picked_vals.append(picked)
 
         def turn_vals(b):
             pairs = picked_vals[b][:].bitcast(F32)
             turned = bank(f"turned{b}", b)
             for u in range(2):
-                nc.tensor.transpose(turned[:, u * P : (u + 1) * P], pairs[:, u : I // 2 : 2], ident[:])
-            grouped = sb([P, P * PACK], BF16, f"val_grouped{b}", tag="val_pool3" if b == 2 else "")
+                nc.tensor.transpose(turned[:, u * P : (u + 1) * P], pairs[:, u : I // 2 : 2], identity[:])
+            grouped = val_grouped[:, b * P * PACK : (b + 1) * P * PACK]
             nc.scalar.copy(
-                grouped[:].bitcast(F32).rearrange("p (e u) -> p e u", u=2),
+                grouped.bitcast(F32).rearrange("p (e u) -> p e u", u=2),
                 turned[:, 0 : 2 * P].rearrange("p (u e) -> p e u", u=2),
             )
-            val_grouped.append(grouped)
 
-        gather_vals(0)
-        gather_vals(1)
+        val_codes = sbuf([P, E], U32, "val_codes", reuse="lower")
+        val_scales = sbuf([P, E], U8, "val_scales")
         for b in range(PACK):
-            if b + 2 < PACK:
-                gather_vals(b + 2)
+            gather_vals(b)
+        val_grouped = sbuf([P, E * PACK], BF16, "val_grouped", reuse="val_pool3")
+        for b in range(PACK):
             turn_vals(b)
 
-        def slot(b):
-            return slice(b * P, (b + 1) * P)
-
         def quantize_vals(b):
+            block = slice(b * P, (b + 1) * P)
             nc.vector.quantize_mx(
-                out=val_codes[:, slot(b)].bitcast(FP8X4), scales=val_scales[:, slot(b)], in_=val_grouped[b][:]
+                out=val_codes[:, block].bitcast(FP8X4), scales=val_scales[:, block], in_=val_grouped[:, b * P * PACK : (b + 1) * P * PACK]
             )
 
-        def product_and_maxima(b):
+        quantize_table(halves[0])
+        quantize_vals(0)
+        quantize_table(halves[1])
+        for b in range(1, PACK):
+            quantize_vals(b)
+
+        result = sbuf([P, PACK, J // RUN], F32, "result")
+        out_rows = out.rearrange("(p b) n -> p b n", b=PACK)
+        for b in range(PACK):
+            block = slice(b * P, (b + 1) * P)
             acc = bank(f"out_acc{b}", PACK + b)
             for cols in halves if b == 0 else (slice(0, J),):
                 nc.tensor.matmul_mx(
                     out=acc[:, cols],
-                    lhsT=val_codes[:, slot(b)].bitcast(FP8X4),
-                    lhsT_scale=val_scales[:, slot(b)],
+                    lhsT=val_codes[:, block].bitcast(FP8X4),
+                    lhsT_scale=val_scales[:, block],
                     rhs=table_codes[:, cols].bitcast(FP8X4),
                     rhs_scale=table_scales[:, cols],
                     start=True,
@@ -240,13 +246,5 @@ def tile_attend_tab_middleof3_bestruns_kernel(
             nc.vector.tensor_reduce(
                 result[:, b, :], acc[:].rearrange("p (n k) -> p n k", k=RUN), mybir.AxisListType.X, ALU.max
             )
-
-        quantize_table(halves[0])
-        quantize_vals(0)
-        quantize_table(halves[1])
-        quantize_vals(1)
-        quantize_vals(2)
-        quantize_vals(3)
-        for b in range(PACK):
-            product_and_maxima(b)
-        nc.sync.dma_start(out.rearrange("(p b) n -> p b n", b=PACK), result[:])
+        nc.sync.dma_start(out_rows[:, : PACK - 1, :], result[:, : PACK - 1, :])
+        nc.sync.dma_start(out_rows[:, PACK - 1, :], result[:, PACK - 1, :])

@@ -22,7 +22,7 @@ BANK = 512
 NOTE_CHUNK = 256
 CHUNKS = U // NOTE_CHUNK
 LINE = 4
-VECTOR_TILES = 2
+VECTOR_SHARE = J // 2
 
 FLOPS = 2 * D * I * U + 2 * I * E * J
 
@@ -83,14 +83,19 @@ def tile_attend_tab_middleof3_bestruns_kernel(
             note_list = sbuf([P, J // LIST_ROWS], U16, f"note_list{k}")
             nc.sync.dma_start(note_list[:], source)
             note_lists.append(note_list)
-        row_factor = sbuf([P, PACK], F32, "row_factor")
-        nc.sync.dma_start(row_factor[:], rowf.rearrange("(p t) one -> p (t one)", t=PACK))
         vals_rows = vals.rearrange("(p b) t -> p b t", b=PACK)
         val_pool = []
         for b in range(PACK):
             pool_block = sbuf([P, T], F32, f"val_pool{b}")
             nc.sync.dma_start(pool_block[:], vals_rows[:, b, :])
             val_pool.append(pool_block)
+
+        row_factor = sbuf([P, PACK], F32, "row_factor")
+        nc.gpsimd.dma_start(row_factor[:], rowf.rearrange("(p t) one -> p (t one)", t=PACK))
+        factor_rows = sbuf([P, PACK, J], F32, "factor_rows")
+        nc.scalar.copy(
+            factor_rows[:], row_factor[:].rearrange("p (t one) -> p t one", one=1).to_broadcast([P, PACK, J])
+        )
 
         identity = sbuf([P, P], F32, "identity")
         make_identity(nc, identity[:])
@@ -147,34 +152,35 @@ def tile_attend_tab_middleof3_bestruns_kernel(
         first = [sbuf([P, J], F32, f"first{t}") for t in range(PACK)]
         second = [sbuf([P, J], F32, f"second{t}") for t in range(PACK)]
         third = [sbuf([P, J], F32, f"third{t}") for t in range(PACK)]
-        scaled = [sbuf([P, J], F32, f"scaled{t}") for t in range(PACK)]
         upper = [sbuf([P, J], F32, f"upper{t}") for t in range(PACK)]
         lower = sbuf([P, PACK, J], F32, "lower")
         capped = sbuf([P, PACK, J], F32, "capped")
         halves = (slice(0, J // 2), slice(J // 2, J))
 
-        def scale_second(t):
-            nc.vector.tensor_scalar(scaled[t][:], second[t][:], row_factor[:, t : t + 1], None, ALU.mult)
+        def scaled_second(t):
+            nc.vector.tensor_tensor(
+                second[t][:], wide[t][:].indirect(note_lists[1][:]), factor_rows[:, t, :], ALU.mult
+            )
 
         def scale_and_compare(dst, looked_up, t, other, op):
             nc.vector.scalar_tensor_tensor(dst, looked_up, row_factor[:, t : t + 1], other, ALU.mult, op)
 
+        scaled_second(0)
+        split = VECTOR_SHARE // LIST_ROWS
+        vector_gather(first[0][:, :VECTOR_SHARE], wide[0][:], note_lists[0][:, :split])
+        scaled_second(1)
+        scalar_gather(first[0][:, VECTOR_SHARE:], wide[0][:], note_lists[0][:, split:])
         for t in range(PACK):
-            gather = vector_gather if t < VECTOR_TILES else scalar_gather
-            gather(second[t][:], wide[t][:], note_lists[1][:])
-            gather(first[t][:], wide[t][:], note_lists[0][:])
-            if t == 0:
-                scale_second(t)
+            if t > 0:
+                scalar_gather(first[t][:], wide[t][:], note_lists[0][:])
             scalar_gather(third[t][:], wide[t][:], note_lists[2][:])
         for t in range(PACK):
-            scale_and_compare(upper[t][:], first[t][:], t, scaled[t][:], ALU.max)
-            scale_and_compare(lower[:, t, :], first[t][:], t, scaled[t][:], ALU.min)
-            if t + 1 < PACK:
-                scale_second(t + 1)
-                scale_and_compare(capped[:, t, :], third[t][:], t, upper[t][:], ALU.min)
-            else:
-                for cols in halves:
-                    scale_and_compare(capped[:, t, cols], third[t][:, cols], t, upper[t][:, cols], ALU.min)
+            scale_and_compare(upper[t][:], first[t][:], t, second[t][:], ALU.max)
+            scale_and_compare(lower[:, t, :], first[t][:], t, second[t][:], ALU.min)
+            if 0 < t < PACK - 1:
+                scaled_second(t + 1)
+            for cols in halves if t == PACK - 1 else (slice(0, J),):
+                scale_and_compare(capped[:, t, cols], third[t][:, cols], t, upper[t][:, cols], ALU.min)
         table = sbuf([P, J, PACK], BF16, "table")
         for cols in halves:
             nc.vector.tensor_tensor(
@@ -193,7 +199,7 @@ def tile_attend_tab_middleof3_bestruns_kernel(
         picked_vals = []
 
         def gather_vals(b):
-            picked = sbuf([P, I], BF16, f"picked_vals{b}", reuse=("first0", "scaled0", "third0", "upper0")[b])
+            picked = sbuf([P, I], BF16, f"picked_vals{b}", reuse=("first0", "second0", "third0", "upper0")[b])
             scalar_gather(picked[:], val_pool[b][:], token_list[:])
             picked_vals.append(picked)
 
@@ -219,7 +225,9 @@ def tile_attend_tab_middleof3_bestruns_kernel(
         def quantize_vals(b):
             block = slice(b * P, (b + 1) * P)
             nc.vector.quantize_mx(
-                out=val_codes[:, block].bitcast(FP8X4), scales=val_scales[:, block], in_=val_grouped[:, b * P * PACK : (b + 1) * P * PACK]
+                out=val_codes[:, block].bitcast(FP8X4),
+                scales=val_scales[:, block],
+                in_=val_grouped[:, b * P * PACK : (b + 1) * P * PACK],
             )
 
         quantize_table(halves[0])

from contextlib import ExitStack

import concourse.mybir as mybir
from concourse.masks import make_identity

F32 = mybir.dt.float32
BF16 = mybir.dt.bfloat16
I32 = mybir.dt.int32
U32 = mybir.dt.uint32
U16 = mybir.dt.uint16
U8 = mybir.dt.uint8
FP8X4 = mybir.dt.float8_e4m3fn_x4
ALU = mybir.AluOpType
COPY = mybir.ActivationFunctionType.Copy

P = 128
PACK = 4
QUADRANTS = 4
LIST_ROWS = 16
D, T, I, J, U, E, RUN = 512, 2048, 512, 512, 1024, 512, 8
BANK = 512
NOTE_CHUNK = 256
CHUNKS = U // NOTE_CHUNK
LINE = 4
VECTOR_SHARE = J // 2

FLOPS = 2 * D * I * U + 2 * I * E * J


def tile_attend_tab_middleof3_bestruns_kernel(
    tc, keys_words, keys_scales, notes, rowf, vals, offs, offs2, offs3, offs4, out
):
    nc = tc.nc
    with ExitStack() as ctx:
        held = ctx.enter_context(tc.tile_pool(name="held", bufs=1))
        psum = ctx.enter_context(tc.psum_pool(name="psum", bufs=1))

        def sbuf(shape, dtype, name, reuse=""):
            return held.tile(shape, dtype, name=name, tag=reuse or name, align_bytes=64)

        def bank(name, number):
            return psum.tile([P, BANK], F32, name=name, tag=f"bank{number}")

        def vector_gather(dst, window, offsets):
            nc.vector.tensor_copy(dst, window.indirect(offsets))

        def scalar_gather(dst, window, offsets):
            nc.scalar.activation(dst, window.indirect(offsets), COPY)

        def by_place(planes):
            return planes.rearrange("p t (c i) -> p c t i", i=LINE)

        def into_words(grouped):
            return grouped.rearrange("p (c i) t -> p c t i", i=LINE)

        notes_rows = notes.rearrange("(p t) u -> p t u", t=PACK)
        note_raw = []

        def load_notes(c):
            raw = sbuf([P, PACK, NOTE_CHUNK], F32, f"note_raw{c}")
            nc.sync.dma_start(raw[:], notes_rows[:, :, c * NOTE_CHUNK : (c + 1) * NOTE_CHUNK])
            note_raw.append(raw)

        load_notes(0)
        token_list = sbuf([P, I // LIST_ROWS], U16, "token_list")
        nc.sync.dma_start(token_list[:], offs)

        key_scales = sbuf([P, T], U8, "key_scales")
        nc.vector.memset(key_scales[:].bitcast(I32), 0)
        for q in range(QUADRANTS):
            nc.sync.dma_start(
                key_scales[32 * q : 32 * q + 4, :].bitcast(I32),
                keys_scales[0, 4 * q : 4 * q + 4, :].bitcast(I32),
            )
        key_words = sbuf([P, T], U32, "key_words")
        nc.sync.dma_start(
            key_words[:].bitcast(I32), keys_words[0].rearrange("p n t -> p (n t)").bitcast(I32)
        )
        for c in range(1, CHUNKS):
            load_notes(c)
        note_lists = []
        for k, source in enumerate((offs2, offs3, offs4)):
            note_list = sbuf([P, J // LIST_ROWS], U16, f"note_list{k}")
            nc.sync.dma_start(note_list[:], source)
            note_lists.append(note_list)
        vals_rows = vals.rearrange("(p b) t -> p b t", b=PACK)
        val_pool = []
        for b in range(PACK):
            pool_block = sbuf([P, T], F32, f"val_pool{b}")
            nc.sync.dma_start(pool_block[:], vals_rows[:, b, :])
            val_pool.append(pool_block)

        row_factor = sbuf([P, PACK], F32, "row_factor")
        nc.gpsimd.dma_start(row_factor[:], rowf.rearrange("(p t) one -> p (t one)", t=PACK))
        factor_rows = sbuf([P, PACK, J], F32, "factor_rows")
        nc.scalar.copy(
            factor_rows[:], row_factor[:].rearrange("p (t one) -> p t one", one=1).to_broadcast([P, PACK, J])
        )

        identity = sbuf([P, P], F32, "identity")
        make_identity(nc, identity[:])

        wide = [sbuf([P, U], F32, f"wide{t}") for t in range(PACK)]
        picked_scales = sbuf([P, I], U8, "picked_scales")
        picked_words = sbuf([P, I], U32, "picked_words")

        def quantize_notes(c):
            grouped = sbuf(
                [P, NOTE_CHUNK, PACK], BF16, f"note_grouped{c}", reuse="note_raw1" if c == 2 else "note_grouped"
            )
            nc.vector.tensor_copy(into_words(grouped[:]), by_place(note_raw[c][:]))
            codes = sbuf([P, NOTE_CHUNK], U32, f"note_codes{c}")
            scales = sbuf([P, NOTE_CHUNK], U8, f"note_scales{c}")
            nc.vector.quantize_mx(
                out=codes[:].bitcast(FP8X4), scales=scales[:], in_=grouped[:].rearrange("p u t -> p (u t)")
            )
            return codes, scales

        def gather_keys():
            vector_gather(picked_scales[:].rearrange("p (t s) -> p s t", t=PACK), key_scales[:], token_list[:])
            vector_gather(picked_words[:].rearrange("p (t s) -> p s t", t=PACK), key_words[:], token_list[:])

        def wide_columns(c, codes, scales, row_tiles, number, copy):
            acc = bank(f"wide_acc{c}_{row_tiles[0]}", number)
            for h, t in enumerate(row_tiles):
                nc.tensor.matmul_mx(
                    out=acc[:, h * NOTE_CHUNK : (h + 1) * NOTE_CHUNK],
                    lhsT=picked_words[:, t * P : (t + 1) * P].bitcast(FP8X4),
                    lhsT_scale=picked_scales[:, t * P : (t + 1) * P],
                    rhs=codes[:].bitcast(FP8X4),
                    rhs_scale=scales[:],
                    start=True,
                    stop=True,
                )
            for h, t in enumerate(row_tiles):
                copy(wide[t][:, c * NOTE_CHUNK : (c + 1) * NOTE_CHUNK], acc[:, h * NOTE_CHUNK : (h + 1) * NOTE_CHUNK])

        for c in range(2):
            codes, scales = quantize_notes(c)
            if c == 0:
                gather_keys()
            wide_columns(c, codes, scales, (0, 1), 2 * c, nc.scalar.copy)
            wide_columns(c, codes, scales, (2, 3), 2 * c + 1, nc.scalar.copy)
        codes, scales = quantize_notes(2)
        wide_columns(2, codes, scales, (0, 1), 4, nc.vector.tensor_copy)
        wide_columns(2, codes, scales, (2, 3), 4, nc.scalar.copy)
        codes, scales = quantize_notes(3)
        wide_columns(3, codes, scales, (0,), 5, nc.vector.tensor_copy)
        wide_columns(3, codes, scales, (1,), 6, nc.vector.tensor_copy)
        wide_columns(3, codes, scales, (2, 3), 7, nc.scalar.copy)

        first = [sbuf([P, J], F32, f"first{t}") for t in range(PACK)]
        second = [sbuf([P, J], F32, f"second{t}") for t in range(PACK)]
        third = [sbuf([P, J], F32, f"third{t}") for t in range(PACK)]
        upper = [sbuf([P, J], F32, f"upper{t}") for t in range(PACK)]
        lower = sbuf([P, PACK, J], F32, "lower")
        capped = sbuf([P, PACK, J], F32, "capped")
        halves = (slice(0, J // 2), slice(J // 2, J))

        def scaled_second(t):
            nc.vector.tensor_tensor(
                second[t][:], wide[t][:].indirect(note_lists[1][:]), factor_rows[:, t, :], ALU.mult
            )

        def scale_and_compare(dst, looked_up, t, other, op):
            nc.vector.scalar_tensor_tensor(dst, looked_up, row_factor[:, t : t + 1], other, ALU.mult, op)

        scaled_second(0)
        split = VECTOR_SHARE // LIST_ROWS
        vector_gather(first[0][:, :VECTOR_SHARE], wide[0][:], note_lists[0][:, :split])
        scaled_second(1)
        scalar_gather(first[0][:, VECTOR_SHARE:], wide[0][:], note_lists[0][:, split:])
        for t in range(PACK):
            if t > 0:
                scalar_gather(first[t][:], wide[t][:], note_lists[0][:])
            scalar_gather(third[t][:], wide[t][:], note_lists[2][:])
        for t in range(PACK):
            scale_and_compare(upper[t][:], first[t][:], t, second[t][:], ALU.max)
            scale_and_compare(lower[:, t, :], first[t][:], t, second[t][:], ALU.min)
            if 0 < t < PACK - 1:
                scaled_second(t + 1)
            for cols in halves if t == PACK - 1 else (slice(0, J),):
                scale_and_compare(capped[:, t, cols], third[t][:, cols], t, upper[t][:, cols], ALU.min)
        table = sbuf([P, J, PACK], BF16, "table")
        for cols in halves:
            nc.vector.tensor_tensor(
                into_words(table[:, cols, :]), by_place(lower[:, :, cols]), by_place(capped[:, :, cols]), ALU.max
            )
        table_codes = sbuf([P, J], U32, "table_codes")
        table_scales = sbuf([P, J], U8, "table_scales")

        def quantize_table(cols):
            nc.vector.quantize_mx(
                out=table_codes[:, cols].bitcast(FP8X4),
                scales=table_scales[:, cols],
                in_=table[:, cols, :].rearrange("p j t -> p (j t)"),
            )

        picked_vals = []

        def gather_vals(b):
            picked = sbuf([P, I], BF16, f"picked_vals{b}", reuse=("first0", "second0", "third0", "upper0")[b])
            scalar_gather(picked[:], val_pool[b][:], token_list[:])
            picked_vals.append(picked)

        def turn_vals(b):
            pairs = picked_vals[b][:].bitcast(F32)
            turned = bank(f"turned{b}", b)
            for u in range(2):
                nc.tensor.transpose(turned[:, u * P : (u + 1) * P], pairs[:, u : I // 2 : 2], identity[:])
            grouped = val_grouped[:, b * P * PACK : (b + 1) * P * PACK]
            nc.scalar.copy(
                grouped.bitcast(F32).rearrange("p (e u) -> p e u", u=2),
                turned[:, 0 : 2 * P].rearrange("p (u e) -> p e u", u=2),
            )

        val_codes = sbuf([P, E], U32, "val_codes", reuse="lower")
        val_scales = sbuf([P, E], U8, "val_scales")
        for b in range(PACK):
            gather_vals(b)
        val_grouped = sbuf([P, E * PACK], BF16, "val_grouped", reuse="val_pool3")
        for b in range(PACK):
            turn_vals(b)

        def quantize_vals(b):
            block = slice(b * P, (b + 1) * P)
            nc.vector.quantize_mx(
                out=val_codes[:, block].bitcast(FP8X4),
                scales=val_scales[:, block],
                in_=val_grouped[:, b * P * PACK : (b + 1) * P * PACK],
            )

        quantize_table(halves[0])
        quantize_vals(0)
        quantize_table(halves[1])
        for b in range(1, PACK):
            quantize_vals(b)

        result = sbuf([P, PACK, J // RUN], F32, "result")
        out_rows = out.rearrange("(p b) n -> p b n", b=PACK)
        for b in range(PACK):
            block = slice(b * P, (b + 1) * P)
            acc = bank(f"out_acc{b}", PACK + b)
            for cols in halves if b == 0 else (slice(0, J),):
                nc.tensor.matmul_mx(
                    out=acc[:, cols],
                    lhsT=val_codes[:, block].bitcast(FP8X4),
                    lhsT_scale=val_scales[:, block],
                    rhs=table_codes[:, cols].bitcast(FP8X4),
                    rhs_scale=table_scales[:, cols],
                    start=True,
                    stop=True,
                )
            nc.vector.tensor_reduce(
                result[:, b, :], acc[:].rearrange("p (n k) -> p n k", k=RUN), mybir.AxisListType.X, ALU.max
            )
        nc.sync.dma_start(out_rows[:, : PACK - 1, :], result[:, : PACK - 1, :])
        nc.sync.dma_start(out_rows[:, PACK - 1, :], result[:, PACK - 1, :])
